import numpy as np
import ml_dtypes

BF16 = ml_dtypes.bfloat16


def bf(x):
    return np.asarray(x, np.float32).astype(BF16)


def f32(x):
    return np.asarray(x, np.float32)


def f64(x):
    return np.asarray(x).astype(np.float64)


def striped(idx):
    return np.concatenate([l.reshape(-1, 16).T for l in idx])


def rows(idx, k):
    return np.tile(np.repeat(idx, 16, axis=0), (k // (16 * 8), 1))


def look(tab, idx):
    return np.take_along_axis(f64(tab), rows(idx, len(tab)), axis=1)


K, S, V, N = 128, 2048, 2048, 2048


def setup_inputs():
    return {"tab": f32(np.random.standard_normal((2, K, S))), "y": f32(np.random.standard_normal((K, V))), "offs": striped(np.stack([np.random.permutation(S)[:N] for _ in range(8)]))}


def reference(tab, y, offs):
    idx = np.stack([g.T.reshape(-1) for g in np.split(offs, 8)])
    x = (look(tab[0], idx) + f64(y)) * (np.maximum(look(tab[1], idx), 0.0))
    return x

@@ -1,0 +1,36 @@
+import concourse.mybir as mybir
+
+F32, U16 = mybir.dt.float32, mybir.dt.uint16
+ADD, MULT = mybir.AluOpType.add, mybir.AluOpType.mult
+RELU = mybir.ActivationFunctionType.Relu
+
+PIECE = 512
+GROUP = 16
+
+
+def tile_lookup_vg_addrelu_out_kernel(tc, tab, y, offs, out):
+    nc = tc.nc
+    rows, places = tab.shape[1], tab.shape[2]
+    entries = y.shape[1]
+    pieces = entries // PIECE
+    with tc.tile_pool(name="held", bufs=1) as held:
+        offsets = held.tile([rows, entries // GROUP], U16, name="offsets")
+        values = held.tile([rows, places], F32, name="values")
+        gates = held.tile([rows, places], F32, name="gates")
+        stream = [held.tile([rows, PIECE], F32, name=f"stream{p}") for p in range(pieces)]
+        summed = [held.tile([rows, PIECE], F32, name=f"summed{p}") for p in range(pieces)]
+        gated = [held.tile([rows, PIECE], F32, name=f"gated{p}") for p in range(pieces)]
+        product = [held.tile([rows, PIECE], F32, name=f"product{p}") for p in range(pieces)]
+
+        nc.sync.dma_start(offsets[:], offs)
+        nc.sync.dma_start(values[:], tab[0])
+        nc.sync.dma_start(gates[:], tab[1])
+        for p in range(pieces):
+            nc.sync.dma_start(stream[p][:], y[:, p * PIECE:(p + 1) * PIECE])
+
+        for p in range(pieces):
+            picks = offsets[:, p * PIECE // GROUP:(p + 1) * PIECE // GROUP]
+            nc.vector.tensor_tensor(summed[p][:], values[:].indirect(picks), stream[p][:], ADD)
+            nc.scalar.activation(gated[p][:], gates[:].indirect(picks), RELU)
+            nc.vector.tensor_tensor(product[p][:], summed[p][:], gated[p][:], MULT)
+            nc.sync.dma_start(out[:, p * PIECE:(p + 1) * PIECE], product[p][:])

@@ -5,6 +5,7 @@ ADD, MULT = mybir.AluOpType.add, mybir.AluOpType.mult
 RELU = mybir.ActivationFunctionType.Relu
 
 PIECE = 512
+EARLY = 2
 GROUP = 16
 
 
@@ -22,15 +23,34 @@ def tile_lookup_vg_addrelu_out_kernel(tc, tab, y, offs, out):
         gated = [held.tile([rows, PIECE], F32, name=f"gated{p}") for p in range(pieces)]
         product = [held.tile([rows, PIECE], F32, name=f"product{p}") for p in range(pieces)]
 
-        nc.sync.dma_start(offsets[:], offs)
+        warm_in = held.tile([rows, GROUP], F32, name="warm_in")
+        warm_out = held.tile([rows, GROUP], F32, name="warm_out")
+
+        def columns(p):
+            return slice(p * PIECE, (p + 1) * PIECE)
+
+        def picks(p):
+            return offsets[:, p * PIECE // GROUP:(p + 1) * PIECE // GROUP]
+
+        def multiply_and_store(p):
+            nc.vector.tensor_tensor(product[p][:], summed[p][:], gated[p][:], MULT)
+            nc.sync.dma_start(out[:, columns(p)], product[p][:])
+
         nc.sync.dma_start(values[:], tab[0])
+        nc.sync.dma_start(offsets[:], offs)
+        for p in range(EARLY):
+            nc.sync.dma_start(stream[p][:], y[:, columns(p)])
         nc.sync.dma_start(gates[:], tab[1])
-        for p in range(pieces):
-            nc.sync.dma_start(stream[p][:], y[:, p * PIECE:(p + 1) * PIECE])
+        for p in range(EARLY, pieces):
+            nc.sync.dma_start(stream[p][:], y[:, columns(p)])
+
+        nc.vector.memset(warm_in[:], 0.0)
+        nc.scalar.activation(warm_out[:], warm_in[:], RELU)
 
         for p in range(pieces):
-            picks = offsets[:, p * PIECE // GROUP:(p + 1) * PIECE // GROUP]
-            nc.vector.tensor_tensor(summed[p][:], values[:].indirect(picks), stream[p][:], ADD)
-            nc.scalar.activation(gated[p][:], gates[:].indirect(picks), RELU)
-            nc.vector.tensor_tensor(product[p][:], summed[p][:], gated[p][:], MULT)
-            nc.sync.dma_start(out[:, p * PIECE:(p + 1) * PIECE], product[p][:])
+            nc.vector.tensor_tensor(summed[p][:], values[:].indirect(picks(p)), stream[p][:], ADD)
+            nc.scalar.activation(gated[p][:], gates[:].indirect(picks(p)), RELU)
+            if p >= EARLY:
+                multiply_and_store(p - EARLY)
+        for p in range(pieces - EARLY, pieces):
+            multiply_and_store(p)

@@ -18,39 +18,34 @@ def tile_lookup_vg_addrelu_out_kernel(tc, tab, y, offs, out):
         offsets = held.tile([rows, entries // GROUP], U16, name="offsets")
         values = held.tile([rows, places], F32, name="values")
         gates = held.tile([rows, places], F32, name="gates")
-        stream = [held.tile([rows, PIECE], F32, name=f"stream{p}") for p in range(pieces)]
-        summed = [held.tile([rows, PIECE], F32, name=f"summed{p}") for p in range(pieces)]
-        gated = [held.tile([rows, PIECE], F32, name=f"gated{p}") for p in range(pieces)]
-        product = [held.tile([rows, PIECE], F32, name=f"product{p}") for p in range(pieces)]
-
+        stream = held.tile([rows, entries], F32, name="stream")
+        summed = held.tile([rows, entries], F32, name="summed")
+        gated = held.tile([rows, entries], F32, name="gated")
+        product = held.tile([rows, entries], F32, name="product")
         warm_in = held.tile([rows, GROUP], F32, name="warm_in")
         warm_out = held.tile([rows, GROUP], F32, name="warm_out")
 
-        def columns(p):
-            return slice(p * PIECE, (p + 1) * PIECE)
-
-        def picks(p):
-            return offsets[:, p * PIECE // GROUP:(p + 1) * PIECE // GROUP]
-
-        def multiply_and_store(p):
-            nc.vector.tensor_tensor(product[p][:], summed[p][:], gated[p][:], MULT)
-            nc.sync.dma_start(out[:, columns(p)], product[p][:])
+        def multiply_and_store(first, width):
+            columns = slice(first, first + width)
+            nc.vector.tensor_tensor(product[:, columns], summed[:, columns], gated[:, columns], MULT)
+            nc.sync.dma_start(out[:, columns], product[:, columns])
 
         nc.sync.dma_start(values[:], tab[0])
         nc.sync.dma_start(offsets[:], offs)
-        for p in range(EARLY):
-            nc.sync.dma_start(stream[p][:], y[:, columns(p)])
+        nc.sync.dma_start(stream[:, :EARLY * PIECE], y[:, :EARLY * PIECE])
         nc.sync.dma_start(gates[:], tab[1])
-        for p in range(EARLY, pieces):
-            nc.sync.dma_start(stream[p][:], y[:, columns(p)])
+        for first in range(EARLY * PIECE, entries, PIECE):
+            nc.sync.dma_start(stream[:, first:first + PIECE], y[:, first:first + PIECE])
 
         nc.vector.memset(warm_in[:], 0.0)
         nc.scalar.activation(warm_out[:], warm_in[:], RELU)
 
         for p in range(pieces):
-            nc.vector.tensor_tensor(summed[p][:], values[:].indirect(picks(p)), stream[p][:], ADD)
-            nc.scalar.activation(gated[p][:], gates[:].indirect(picks(p)), RELU)
+            columns = slice(p * PIECE, (p + 1) * PIECE)
+            picks = offsets[:, p * PIECE // GROUP:(p + 1) * PIECE // GROUP]
+            nc.vector.tensor_tensor(summed[:, columns], values[:].indirect(picks), stream[:, columns], ADD)
+            nc.scalar.activation(gated[:, columns], gates[:].indirect(picks), RELU)
             if p >= EARLY:
-                multiply_and_store(p - EARLY)
-        for p in range(pieces - EARLY, pieces):
-            multiply_and_store(p)
+                multiply_and_store((p - EARLY) * PIECE, PIECE)
+        for first in range((pieces - EARLY) * PIECE, entries, PIECE // 2):
+            multiply_and_store(first, PIECE // 2)

import concourse.mybir as mybir

F32, U16 = mybir.dt.float32, mybir.dt.uint16
ADD, MULT = mybir.AluOpType.add, mybir.AluOpType.mult
RELU = mybir.ActivationFunctionType.Relu

PIECE = 512
EARLY = 2
GROUP = 16


def tile_lookup_vg_addrelu_out_kernel(tc, tab, y, offs, out):
    nc = tc.nc
    rows, places = tab.shape[1], tab.shape[2]
    entries = y.shape[1]
    pieces = entries // PIECE
    with tc.tile_pool(name="held", bufs=1) as held:
        offsets = held.tile([rows, entries // GROUP], U16, name="offsets")
        values = held.tile([rows, places], F32, name="values")
        gates = held.tile([rows, places], F32, name="gates")
        stream = held.tile([rows, entries], F32, name="stream")
        summed = held.tile([rows, entries], F32, name="summed")
        gated = held.tile([rows, entries], F32, name="gated")
        product = held.tile([rows, entries], F32, name="product")
        warm_in = held.tile([rows, GROUP], F32, name="warm_in")
        warm_out = held.tile([rows, GROUP], F32, name="warm_out")

        def multiply_and_store(first, width):
            columns = slice(first, first + width)
            nc.vector.tensor_tensor(product[:, columns], summed[:, columns], gated[:, columns], MULT)
            nc.sync.dma_start(out[:, columns], product[:, columns])

        nc.sync.dma_start(values[:], tab[0])
        nc.sync.dma_start(offsets[:], offs)
        nc.sync.dma_start(stream[:, :EARLY * PIECE], y[:, :EARLY * PIECE])
        nc.sync.dma_start(gates[:], tab[1])
        for first in range(EARLY * PIECE, entries, PIECE):
            nc.sync.dma_start(stream[:, first:first + PIECE], y[:, first:first + PIECE])

        nc.vector.memset(warm_in[:], 0.0)
        nc.scalar.activation(warm_out[:], warm_in[:], RELU)

        for p in range(pieces):
            columns = slice(p * PIECE, (p + 1) * PIECE)
            picks = offsets[:, p * PIECE // GROUP:(p + 1) * PIECE // GROUP]
            nc.vector.tensor_tensor(summed[:, columns], values[:].indirect(picks), stream[:, columns], ADD)
            nc.scalar.activation(gated[:, columns], gates[:].indirect(picks), RELU)
            if p >= EARLY:
                multiply_and_store((p - EARLY) * PIECE, PIECE)
        for first in range((pieces - EARLY) * PIECE, entries, PIECE // 2):
            multiply_and_store(first, PIECE // 2)
